import numpy as np
import ml_dtypes


def mxq(x, axis, fmt="e4m3"):
    dtype, down = {"e4m3": (ml_dtypes.float8_e4m3fn, 7), "e5m2": (ml_dtypes.float8_e5m2, 14)}[fmt]
    v = np.moveaxis(np.asarray(x, np.float32).astype(ml_dtypes.bfloat16).astype(np.float64), axis, -1)
    blocks = v.reshape(v.shape[:-1] + (-1, 32))
    amax = np.abs(blocks).max(-1, keepdims=True)
    byte = np.maximum(np.where(amax > 0, np.frexp(amax)[1] - 1 + 127, 0) - down, 1)
    scale = np.exp2(byte - 127.0)
    codes = (blocks / scale).astype(np.float32).astype(dtype).astype(np.float64)
    return np.moveaxis((codes * scale).reshape(v.shape), -1, axis)


WIDE = False


def mx_kscale(k):
    if not WIDE:
        return np.ones(k)
    levels = np.array([10, -10, 5, -5, 0])
    if k % 512:
        return np.exp2(np.random.permutation(np.resize(levels, k // 32))).repeat(32)
    a = np.empty((k // 512, 16))
    for p in range(k // 512):
        a[p, :8] = np.random.permutation(np.resize(levels, 8))
        for g in range(8):
            far = levels[np.abs(levels - a[p, g]) >= 10]
            a[p, g + 8] = far[np.random.randint(len(far))]
    return np.exp2(a.ravel()).repeat(32)


BF16 = ml_dtypes.bfloat16


def bf(x):
    return np.asarray(x, np.float32).astype(BF16)


def f64(x):
    return np.asarray(x).astype(np.float64)


B, H, T, S, E = 2, 2, 512, 1024, 512
D = H * E
EPS = 1e-5


def draw0():
    s, t, r = mx_kscale(E), mx_kscale(S), mx_kscale(D)
    q = np.random.standard_normal((B, H, T, E)) * s
    k = np.random.standard_normal((B, H, S, E)) / s
    rab = 0.8 * np.random.standard_normal((H, T, S))
    c = (1.0 + 0.1 * np.random.standard_normal(S)) * t
    v = np.random.standard_normal((B, H, S, E)) + 0.5 * np.random.standard_normal((B, H, S, 1))
    v = v * (0.02 / np.sqrt(S)) / t[:, None]
    x = np.random.standard_normal((B, T, D)) * r
    wu = np.random.standard_normal((D, D)) / np.sqrt(D) / r[:, None]
    return {"q": bf(q), "k": bf(k), "rab": bf(rab), "c": bf(c), "v": bf(v), "x": bf(x), "wu": bf(wu)}


def sigmoid(z):
    return 1.0 / (1.0 + np.exp(-z))


def silu_gate(z):
    return z * sigmoid(z)


def plain_layer_norm(p):
    mean = np.mean(p, axis=-1, keepdims=True)
    centered = p - mean
    var = np.mean(centered * centered, axis=-1, keepdims=True)
    return centered / np.sqrt(var + EPS)


def core(q, k, rab, c, v, x, wu):
    b, h, t, e = q.shape
    qq = mxq(f64(q), 3, "e4m3")
    kq = mxq(f64(k), 3, "e4m3")
    l = (qq @ kq.transpose(0, 1, 3, 2)) / np.sqrt(e) + f64(rab)[None, :, :, :]
    a = f64(c)[None, None, None, :] * l * sigmoid(l)
    o = mxq(a, 3, "e4m3") @ mxq(f64(v), 2, "e4m3")
    p = np.transpose(o, (0, 2, 1, 3)).reshape(b, t, h * e)
    n = plain_layer_norm(p)
    u = silu_gate(mxq(f64(x), 2, "e4m3") @ mxq(f64(wu), 0, "e4m3"))
    return n * u


def e4m3fn_bytes(y):
    return np.clip(np.asarray(y, np.float64), -448.0, 448.0).astype(np.float32).astype(ml_dtypes.float8_e4m3fn).view(np.uint8)


def e4m3fn_values(b):
    return np.asarray(b, np.uint8).view(ml_dtypes.float8_e4m3fn).astype(np.float64)


def setup_inputs():
    d = draw0()
    x0 = np.asarray(d['v']).astype(np.float64)
    s = (np.max(np.abs(x0), axis=(0, 1, 3), keepdims=True) / 448.0).astype(np.float32)
    out = {}
    for k, v in d.items():
        if k == 'v':
            out['v_bytes'] = e4m3fn_bytes(x0 / s.astype(np.float64))
            out['v_scale'] = s
        else:
            out[k] = v
    return out


def reference(q, k, rab, c, v_bytes, v_scale, x, wu):
    return core(q, k, rab, c, e4m3fn_values(v_bytes) * v_scale.astype(np.float64), x, wu)

from contextlib import ExitStack

import concourse.mybir as mybir
from concourse.masks import make_identity

F32 = mybir.dt.float32
BF16 = mybir.dt.bfloat16
U32 = mybir.dt.uint32
U8 = mybir.dt.uint8
FP8 = mybir.dt.float8_e4m3fn
FP8X4 = mybir.dt.float8_e4m3fn_x4
ALU = mybir.AluOpType
ACT = mybir.ActivationFunctionType

P = 128
B, H, T, S, E = 2, 2, 512, 1024, 512
D = H * E
EPS = 1e-5
UNITS = B * H * 2
FLOPS = 2 * (2 * B * H * T * S * E + B * T * D * D)


def tile_hstupointwisetransducer_kernel(tc, q, k, rab, c, v_bytes, v_scale, x, wu, out):
    nc = tc.nc
    inv = 1.0 / float(E) ** 0.5

    q_hbm = q.rearrange("b h (r i) e -> b h r i e", i=4)
    k_v = k.rearrange("b h (g m j) e -> b h g m j e", g=2, j=4)
    rab_v = rab.rearrange("h (r i) s -> h r i s", i=4)
    vb_v = v_bytes.rearrange("b h (g p j) f -> b h g p j f", g=2, j=4)
    x_v = x.rearrange("b (r i) d -> b r i d", i=4)
    wu_v = wu.rearrange("(g p j) n -> g p j n", g=2, j=4)
    out_v = out.rearrange("b (r i) d -> b r i d", i=4)

    with ExitStack() as ctx:
        sb = ctx.enter_context(tc.tile_pool(name="sb", bufs=1))
        ps = ctx.enter_context(tc.psum_pool(name="ps", bufs=1))

        ident = sb.tile([P, P], F32, name="ident")
        make_identity(nc, ident[:])
        mhalf = sb.tile([P, 1], F32, name="mhalf")
        nc.gpsimd.memset(mhalf[:], -0.5)
        dummy = sb.tile([P, 1], F32, name="dummy")
        nc.vector.memset(dummy[:], 0.0)
        c_sb = sb.tile([P, 2, 4], BF16, name="c_sb")
        vs_sb = sb.tile([P, 2, 4], F32, name="vs_sb")

        st = {}
        v_copy = nc.vector.tensor_copy
        s_copy = nc.scalar.copy

        def grp(name):
            return sb.tile([P, 2048], BF16, name=name, tag="grp", bufs=5, align_bytes=64)

        def codes(name, tag, bufs):
            cd = sb.tile([P, 512], U32, name=name, tag=tag, bufs=bufs, align_bytes=64)
            sc = sb.tile([P, 512], U8, name=name + "_s", tag=tag + "_s", bufs=bufs, align_bytes=64)
            return cd, sc

        def quant(cs, src):
            nc.vector.quantize_mx(out=cs[0][:].bitcast(FP8X4), scales=cs[1][:], in_=src[:])

        def bank(tag, bufs):
            return ps.tile([P, 512], F32, name=tag, tag=tag, bufs=bufs)

        def ld_k(i):
            t = sb.tile([P, 4, E], BF16, name="k_in", tag="k_in", bufs=3)
            nc.sync.dma_start(out=t[:], in_=k_v[i // 4, (i // 2) % 2, i % 2])
            st["kin", i] = t

        def ld_q(n):
            t = sb.tile([P, 4, E], BF16, name="q_in", tag="q_in", bufs=2)
            nc.sync.dma_start(out=t[:], in_=q_hbm[n // 2, n % 2])
            st["qin", n] = t

        def ld_r(h, g):
            t = sb.tile([P, 4, 512], BF16, name="r_in", tag="r_in", bufs=2)
            nc.sync.dma_start(out=t[:], in_=rab_v[h][:, :, g * 512:(g + 1) * 512])
            st["rin", h, g] = t

        def ld_v(i):
            t = sb.tile([P, 4, E], U8, name="v_in", tag="v_in", bufs=3)
            nc.sync.dma_start(out=t[:], in_=vb_v[i // 4, (i // 2) % 2, i % 2])
            st["vin", i] = t

        def ld_x(b):
            t = sb.tile([P, 4, D], BF16, name="x_in", tag="x_in", bufs=1)
            nc.sync.dma_start(out=t[:], in_=x_v[b])
            st["xin", b] = t

        def ld_w(g, n):
            t = sb.tile([P, 4, 512], BF16, name="w_in", tag="w_in", bufs=3)
            nc.sync.dma_start(out=t[:], in_=wu_v[g][:, :, n * 512:(n + 1) * 512])
            st["win", g, n] = t

        def t_rows(src, words0, key, on_v=()):
            g_t = grp("grp_" + key[0])
            g_w = g_t[:].bitcast(F32).rearrange("p (s r u) -> p s r u", s=4, u=2)
            for hb in range(2):
                bk = bank("tp", 2)
                for sl in range(2):
                    for u in range(2):
                        s = 2 * sl + u
                        nc.tensor.transpose(bk[:, s * P:(s + 1) * P], src(2 * hb + sl)[:, words0 + u:words0 + 256:2], ident[:])
                (v_copy if hb in on_v else s_copy)(
                    out=g_w[:, 2 * hb:2 * hb + 2],
                    in_=bk[:].rearrange("p (s u r) -> p s r u", s=2, u=2),
                )
            st[key] = g_t

        def t_k(i, on_v=()):
            t = st.pop(("kin", i))
            t_rows(lambda s: t[:, s, :].bitcast(F32), 0, ("kg", i), on_v)

        def t_q(n, on_v=()):
            t = st.pop(("qin", n))
            t_rows(lambda s: t[:, s, :].bitcast(F32), 0, ("qg", n), on_v)

        def t_x(b, g):
            t = st["xin", b]
            t_rows(lambda s: t[:, s, :].bitcast(F32), 256 * g, ("xg", b, g))

        def t_r(h, g, on_v=()):
            t = st.pop(("rin", h, g))
            r_t = sb.tile([P, 2, 512], F32, name="rT", tag="rT", bufs=4)
            for u in range(2):
                bk = bank("tp", 2)
                for i in range(4):
                    nc.tensor.transpose(bk[:, i * P:(i + 1) * P], t[:, i, :].bitcast(F32)[:, u:256:2], ident[:])
                (v_copy if u in on_v else s_copy)(out=r_t[:, u, :], in_=bk[:])
            st["rT", h, g] = r_t

        def q_k(i):
            cs = codes("kc", "kc", 2)
            quant(cs, st.pop(("kg", i)))
            st["kc", i] = cs

        def q_q(n):
            cs = codes("qc", "qc", 2)
            quant(cs, st.pop(("qg", n)))
            st["qc", n] = cs

        def q_x(b, g):
            cs = codes("xc", "xc", 4)
            quant(cs, st.pop(("xg", b, g)))
            st["xc", b, g] = cs

        def interleave(eng_copy, dst, src):
            eng_copy(
                out=dst.rearrange("p (c i j) -> p c j i", i=4, j=4),
                in_=src.rearrange("p j (c i) -> p c j i", i=4),
            )

        def il_w(g, n, eng_copy):
            t = st.pop(("win", g, n))
            w_t = grp("grp_w")
            interleave(eng_copy, w_t[:], t[:])
            st["wg", g, n] = w_t

        def q_w(g, n):
            cs = codes("wc", "wc", 4)
            quant(cs, st.pop(("wg", g, n)))
            st["wc", g, n] = cs

        def w_v(i):
            t = st.pop(("vin", i))
            vp = sb.tile([P, 4, E], BF16, name="vp", tag="vp", bufs=2)
            for j in range(4):
                nc.scalar.activation(out=vp[:, j, :], in_=t[:, j, :].bitcast(FP8), func=ACT.Copy, scale=vs_sb[:, i % 2, j:j + 1])
            st["vp", i] = vp

        def il_v(i):
            t = st.pop(("vp", i))
            v_t = grp("grp_v")
            interleave(s_copy if i in (6,) else v_copy, v_t[:], t[:])
            st["vg", i] = v_t

        def q_v(i):
            cs = codes("vc", "vc", 8)
            quant(cs, st.pop(("vg", i)))
            st["vc", i] = cs

        def mx(o, lc, lcols, rc, start, stop):
            nc.tensor.matmul_mx(
                out=o,
                lhsT=lc[0][:, lcols:lcols + P].bitcast(FP8X4),
                lhsT_scale=lc[1][:, lcols:lcols + P],
                rhs=rc[0][:].bitcast(FP8X4),
                rhs_scale=rc[1][:],
                start=start,
                stop=stop,
            )

        def mm_s(i):
            banks = []
            for j in range(4):
                bk = bank("sc", 4)
                mx(bk[:], st["kc", i], P * j, st["qc", i // 2], True, True)
                banks.append(bk)
            st["sc", i] = banks

        def ab(i):
            h, g = (i // 2) % 2, i % 2
            banks = st.pop(("sc", i))
            r_b = st["rT", h, g]
            l_t = sb.tile([P, 4, 512], F32, name="l", tag="l", bufs=2)
            for j in range(4):
                nc.vector.scalar_tensor_tensor(
                    out=l_t[:, j, :],
                    in0=banks[j][:],
                    scalar=inv,
                    in1=r_b[:, j // 2, :].bitcast(BF16)[:, j % 2:1024:2],
                    op0=ALU.mult,
                    op1=ALU.add,
                )
                nc.scalar.activation(out=l_t[:, j, :], in_=l_t[:, j, :], func=ACT.Silu)
            st["l", i] = l_t

        def c_a(i):
            g = i % 2
            l_t = st.pop(("l", i))
            a_t = sb.tile([P, 2048], BF16, name="ag", tag="ag", bufs=2, align_bytes=64)
            nc.vector.tensor_tensor(
                out=a_t[:].rearrange("p (c i j) -> p c j i", i=4, j=4),
                in0=l_t[:].rearrange("p j (c i) -> p c j i", i=4),
                in1=c_sb[:, g, :].unsqueeze(1).unsqueeze(3).to_broadcast([P, P, 4, 4]),
                op=ALU.mult,
            )
            st["ag", i] = a_t

        def q_a(i):
            cs = codes("ac", "ac", 8)
            quant(cs, st.pop(("ag", i)))
            st["ac", i] = cs

        def gate(b, t, tag="tp"):
            u_t = sb.tile([P, D], F32, name="u", tag="u", bufs=5)
            for n in range(2):
                bk = bank(tag, 2)
                for g in range(2):
                    mx(bk[:], st["xc", b, g], P * t, st["wc", g, n], g == 0, g == 1)
                nc.scalar.activation(out=u_t[:, n * 512:(n + 1) * 512], in_=bk[:], func=ACT.Silu)
            st["u", b, t] = u_t

        def o_mm(b, t, tag, bufs, last):
            if ("o", b, t) not in st:
                st["o", b, t] = [bank(tag, bufs), bank(tag, bufs)]
                todo = [(0, 0), (0, 1), (1, 0)]
            else:
                todo = []
            if last:
                todo.append((1, 1))
            for h, g in todo:
                i = 4 * b + 2 * h + g
                mx(st["o", b, t][h][:], st["ac", i], P * t, st["vc", i], g == 0, g == 1)

        def stat(b, t, h):
            if h == 0:
                st["s6", b, t] = sb.tile([P, 12], F32, name="s6", tag="s6", bufs=4)
            nc.vector.bn_stats(out=st["s6", b, t][:, 6 * h:6 * h + 6], in_=st["o", b, t][h][:])

        def aggr(b, t):
            mv = sb.tile([P, 2], F32, name="mv", tag="mv", bufs=4)
            ve = sb.tile([P, 1], F32, name="ve", tag="ve", bufs=4)
            rs = sb.tile([P, 1], F32, name="rs", tag="rs", bufs=4)
            nc.vector.bn_aggr(out=mv[:], in_=st.pop(("s6", b, t))[:])
            nc.gpsimd.tensor_scalar(out=ve[:], in0=mv[:, 1:2], scalar1=EPS, scalar2=None, op0=ALU.add)
            nc.gpsimd.tensor_tensor(out=rs[:], in0=ve[:], in1=mhalf[:], op=ALU.pow)
            st["mv", b, t] = (mv, rs)

        def final(b, t, scale, split, via_s=()):
            banks = st.pop(("o", b, t))
            mv, rs = st.pop(("mv", b, t))
            u_t = st.pop(("u", b, t))
            w_t = sb.tile([P, D], F32, name="w", tag="w", bufs=3)
            for h in range(2):
                sl = slice(h * 512, (h + 1) * 512)
                if h in via_s:
                    nb = sb.tile([P, 1], F32, name="nb", tag="nb", bufs=4)
                    nc.gpsimd.tensor_scalar(out=nb[:], in0=mv[:, 0:1], scalar1=-1.0, scalar2=rs[:, 0:1], op0=ALU.mult, op1=ALU.mult)
                    nc.scalar.activation(out=w_t[:, sl], in_=banks[h][:], func=ACT.Identity, scale=rs[:, 0:1], bias=nb[:, 0:1])
                    nc.gpsimd.tensor_tensor(out=w_t[:, sl], in0=w_t[:, sl], in1=u_t[:, sl], op=ALU.mult)
                    continue
                nc.vector.scalar_tensor_tensor(
                    out=w_t[:, sl], in0=banks[h][:], scalar=mv[:, 0:1], in1=u_t[:, sl], op0=ALU.subtract, op1=ALU.mult
                )
                if scale == "s":
                    nc.scalar.activation(out=w_t[:, sl], in_=w_t[:, sl], func=ACT.Copy, scale=rs[:, 0:1])
                elif scale == "v":
                    nc.vector.tensor_scalar(out=w_t[:, sl], in0=w_t[:, sl], scalar1=rs[:, 0:1], scalar2=None, op0=ALU.mult)
                else:
                    nc.gpsimd.tensor_scalar(
                        out=w_t[:, sl], in0=w_t[:, sl], scalar1=rs[:, 0:1], scalar2=0.0, op0=ALU.mult, op1=ALU.add
                    )
            if split:
                for h in range(2):
                    sl = slice(h * 512, (h + 1) * 512)
                    nc.sync.dma_start(out=out_v[b][:, t, sl], in_=w_t[:, sl])
            else:
                nc.sync.dma_start(out=out_v[b][:, t, :], in_=w_t[:])

        nc.scalar.dma_start(out=vs_sb[:], in_=v_scale.rearrange("o a (g p j) z -> p (o a g) (j z)", g=2, j=4))
        nc.scalar.dma_start(out=c_sb[:], in_=c.rearrange("(g p j) -> p g j", g=2, j=4))
        nc.scalar.activation(out=dummy[:], in_=dummy[:], func=ACT.Silu)
        ld_w(0, 0)
        ld_q(0)
        ld_k(0)
        ld_r(0, 0)
        ld_w(0, 1)
        ld_k(1)
        ld_v(0)
        ld_r(0, 1)
        il_w(0, 0, v_copy)
        t_q(0, (1,))
        t_k(0, (1,))
        q_q(0)
        q_w(0, 0)
        q_k(0)
        t_r(0, 0, (1,))
        mm_s(0)
        t_k(1)
        ld_q(1)
        ld_k(2)
        ld_v(1)
        ld_r(1, 0)
        ld_w(1, 0)
        ld_k(3)
        ld_v(2)
        ld_w(1, 1)
        w_v(0)
        t_r(0, 1)
        ld_r(1, 1)
        ld_x(0)
        late = {
            0: lambda: (ld_q(2), ld_k(4), ld_v(3)),
            1: lambda: (ld_k(5), ld_v(4)),
            2: lambda: (ld_q(3), ld_k(6), ld_v(5), ld_x(1)),
            3: lambda: (ld_k(7), ld_v(6)),
            4: lambda: (ld_v(7),),
        }
        for i in range(UNITS):
            ab(i)
            if i + 1 < UNITS:
                q_k(i + 1)
                if i % 2 == 1:
                    q_q((i + 1) // 2)
                mm_s(i + 1)
            if i == 3:
                q_x(0, 0)
                q_x(0, 1)
            if i == 5:
                q_x(1, 0)
                q_x(1, 1)
            if i >= 4:
                o_mm(0, i - 4, "og", 2, True)
                stat(0, i - 4, 0)
                stat(0, i - 4, 1)
                aggr(0, i - 4)
            il_v(i)
            if i == 0:
                il_w(0, 1, v_copy)
            if i == 2:
                il_w(1, 1, s_copy)
            if i + 2 < UNITS:
                t_k(i + 2)
                if i % 2 == 0:
                    t_q((i + 2) // 2)
                if i + 2 < 4:
                    t_r(1, i % 2)
            if i + 1 < UNITS:
                w_v(i + 1)
            if i in late:
                late[i]()
            if i == 1:
                il_w(1, 0, s_copy)
            if i in (2, 4):
                t_x(i // 4, 0)
                t_x(i // 4, 1)
            c_a(i)
            q_v(i)
            if i == 0:
                q_w(0, 1)
            if i == 2:
                q_w(1, 0)
            if i == 3:
                q_w(1, 1)
            q_a(i)
            if i >= 4:
                final(0, i - 4, "s", False)
            if 3 <= i <= 6:
                gate(0, i - 3, "og")
            if i == 6:
                gate(1, 0, "og")
            if i == 7:
                gate(1, 1, "og")
        for t in range(4):
            tag, bufs = (("sc", 4), ("sc", 4), ("tp", 2), ("og", 2))[t]
            o_mm(1, t, tag, bufs, True)
            stat(1, t, 0)
            stat(1, t, 1)
            aggr(1, t)
            if t < 2:
                gate(1, t + 2, "og")
            final(1, t, "s", t == 3, ((), (), (), ())[t])
